import numpy as np
import ml_dtypes


def mxq(x, axis, fmt="e4m3"):
    dtype, down = {"e4m3": (ml_dtypes.float8_e4m3fn, 7), "e5m2": (ml_dtypes.float8_e5m2, 14)}[fmt]
    v = np.moveaxis(np.asarray(x, np.float32).astype(ml_dtypes.bfloat16).astype(np.float64), axis, -1)
    blocks = v.reshape(v.shape[:-1] + (-1, 32))
    amax = np.abs(blocks).max(-1, keepdims=True)
    byte = np.maximum(np.where(amax > 0, np.frexp(amax)[1] - 1 + 127, 0) - down, 1)
    scale = np.exp2(byte - 127.0)
    codes = (blocks / scale).astype(np.float32).astype(dtype).astype(np.float64)
    return np.moveaxis((codes * scale).reshape(v.shape), -1, axis)


WIDE = False


def mx_kscale(k):
    if not WIDE:
        return np.ones(k)
    levels = np.array([10, -10, 5, -5, 0])
    if k % 512:
        return np.exp2(np.random.permutation(np.resize(levels, k // 32))).repeat(32)
    a = np.empty((k // 512, 16))
    for p in range(k // 512):
        a[p, :8] = np.random.permutation(np.resize(levels, 8))
        for g in range(8):
            far = levels[np.abs(levels - a[p, g]) >= 10]
            a[p, g + 8] = far[np.random.randint(len(far))]
    return np.exp2(a.ravel()).repeat(32)


def f64(x):
    return np.asarray(x).astype(np.float64)


def striped(idx):
    return np.tile(idx.reshape(-1, 16).T, (8, 1)).astype(np.uint16)


def unstriped(offs):
    return offs[:16].T.reshape(-1).astype(np.int64)


def striped8(idx):
    return np.concatenate([x.reshape(-1, 16).T for x in idx]).astype(np.uint16)


def runs(offs, k):
    lists = np.stack([offs[16 * r : 16 * r + 16].T.reshape(-1) for r in range(8)]).astype(np.int64)
    return lists[np.arange(k) % 512 // 64]


def pack_weight(w):
    k, n = w.shape
    w = f64(np.asarray(w, np.float32).astype(ml_dtypes.bfloat16)).reshape(k // 32, 32, n)
    amax = np.abs(w).max(1)
    byte = np.clip(np.where(amax > 0, np.frexp(amax)[1] - 1 + 127 - 7, 1), 1, 254)
    scaled = (w * np.exp2(127.0 - byte)[:, None, :]).reshape(k, n).astype(np.float32)
    words = np.ascontiguousarray(scaled.reshape(k // 512, 128, 4, n).transpose(0, 1, 3, 2)).astype(ml_dtypes.float8_e4m3fn).view(np.uint8)
    return words, np.ascontiguousarray(byte.astype(np.uint8).reshape(k // 512, 16, n))


def unpack_weight(words, scales):
    g, p, n, _ = words.shape
    vals = np.ascontiguousarray(words).view(ml_dtypes.float8_e4m3fn).astype(np.float64) * np.repeat(np.exp2(scales.astype(np.float64) - 127.0), 8, axis=1)[..., None]
    return vals.transpose(0, 1, 3, 2).reshape(g * 512, n)


K, T, S, H, C, W = 512, 2048, 256, 512, 512, 128


def setup_inputs():
    n = np.random.standard_normal
    s = mx_kscale(K)[:, None]
    packed_xT = pack_weight(n((K, T)) * s)
    packed_w1 = pack_weight(n((K, H)) / np.sqrt(2 * K) / s)
    packed_w2 = pack_weight(n((K, H)) / np.sqrt(2 * K) / s)
    perm = np.random.permutation(S)
    return {
        "x_words": packed_xT[0],
        "x_scales": packed_xT[1],
        "w1_words": packed_w1[0],
        "w1_scales": packed_w1[1],
        "w2_words": packed_w2[0],
        "w2_scales": packed_w2[1],
        "gs": (np.random.uniform(0.5, 1.5, (K, 1)) / s).astype(np.float32),
        "offs": striped(np.random.permutation(T)[:S]),
        "hz": striped8(np.random.randint(0, T, (8, S))),
        "n1": striped(np.random.permutation(S)),
        "n2": striped(np.random.permutation(S)),
        "cand": striped8(np.random.randint(0, T, (8, C))),
        "n3": striped(perm[:W]),
        "n4": striped(perm[W:]),
    }


def reference(x_words, x_scales, w1_words, w1_scales, w2_words, w2_scales, gs, offs, hz, n1, n2, cand, n3, n4):
    x_cand = unpack_weight(x_words, x_scales)[np.arange(K)[:, None], runs(cand, K)]
    xq = unpack_weight(x_words, x_scales)[:, unstriped(offs)]
    x_hz = unpack_weight(x_words, x_scales)[np.arange(K)[:, None], runs(hz, K)]
    y = unpack_weight(w1_words, w1_scales).T @ xq + unpack_weight(w2_words, w2_scales).T @ x_hz
    ds = np.zeros((H, S))
    ds[:, unstriped(n1)] = y
    st = np.maximum(y, ds)
    ds2 = np.zeros((H, S))
    ds2[:, unstriped(n2)] = st
    z = f64(gs) * (st - ds2)
    s = 0.0625 * ((x_cand.T @ mxq(z, 0, "e4m3")))
    pa = s[:, unstriped(n3)]
    pb = s[:, unstriped(n4)]
    ra = np.maximum(pa, pb)
    out = s.copy()
    out[:, unstriped(n3)] = ra
    return out

from contextlib import ExitStack

import concourse.mybir as mybir

K, T, S, H, C, W = 512, 2048, 256, 512, 512, 128
FLOPS = 2 * K * H * S * 2 + 2 * K * C * S

F32 = mybir.dt.float32
BF16 = mybir.dt.bfloat16
I32 = mybir.dt.int32
U32 = mybir.dt.uint32
U16 = mybir.dt.uint16
U8 = mybir.dt.uint8
FP8X4 = mybir.dt.float8_e4m3fn_x4
ALU = mybir.AluOpType
COPY = mybir.ActivationFunctionType.Copy

P = 128
PACK = 4
ROW_STEP = 8
QUADRANT = 32


def as_words(packed):
    return packed[0].rearrange("p n t -> p (n t)").bitcast(I32)


def move_scale_rows(queue, plane, spread):
    for i in range(1, 4):
        queue.dma_start(
            out=plane[:].bitcast(I32)[i:P:QUADRANT, :],
            in_=spread[:].bitcast(I32)[ROW_STEP * i : P : QUADRANT, :],
        )


def tile_picked_dthzksndtwinfill_none_p_kernel(
    tc, x_words, x_scales, w1_words, w1_scales, w2_words, w2_scales, gs, offs, hz, n1, n2, cand, n3, n4, out
):
    nc = tc.nc
    with ExitStack() as ctx:
        keep = ctx.enter_context(tc.tile_pool(name="keep", bufs=1))
        psum = ctx.enter_context(tc.psum_pool(name="psum", bufs=1))

        def load_list(name, source):
            tile = keep.tile(list(source.shape), U16, name=name)
            nc.sync.dma_start(tile[:], source)
            return tile

        xs_rows = keep.tile([P, T], U8, align_bytes=64)
        nc.vector.memset(xs_rows[:].bitcast(I32), 0)
        ws_rows = keep.tile([P, 2 * H], U8, align_bytes=64)
        nc.vector.memset(ws_rows[:].bitcast(I32), 0)
        hz_list = load_list("hz_list", hz)
        offs_list = load_list("offs_list", offs)
        w1_raw = keep.tile([P, H], U32, tag="w1_raw_then_gain", align_bytes=64)
        nc.sync.dma_start(out=w1_raw[:].bitcast(I32), in_=as_words(w1_words))
        nc.sync.dma_start(out=xs_rows[:].bitcast(I32)[0:P:ROW_STEP, :], in_=x_scales[0].bitcast(I32))
        for half, scales in enumerate((w1_scales, w2_scales)):
            nc.sync.dma_start(
                out=ws_rows[:, half * H : (half + 1) * H].bitcast(I32)[0:P:ROW_STEP, :], in_=scales[0].bitcast(I32)
            )
        n1_list = load_list("n1_list", n1)
        x_table = keep.tile([P, T], U32, align_bytes=64)
        nc.sync.dma_start(out=x_table[:].bitcast(I32), in_=as_words(x_words))
        w2_raw = keep.tile([P, H], U32, align_bytes=64)
        nc.sync.dma_start(out=w2_raw[:].bitcast(I32), in_=as_words(w2_words))

        picked_bytes = keep.tile([P, 2 * S], U8, align_bytes=64)
        nc.vector.tensor_copy(picked_bytes[:, 0:S], xs_rows[:].indirect(offs_list[:]))
        nc.vector.tensor_copy(picked_bytes[:, S : 2 * S], xs_rows[:].indirect(hz_list[:]))
        picked_scale = keep.tile([P, 2 * S], U8, align_bytes=64)
        nc.vector.tensor_copy(picked_scale[:].bitcast(I32), picked_bytes[:].bitcast(I32))
        move_scale_rows(nc.sync, picked_scale, picked_bytes)

        ws_dealt = keep.tile([P, 2 * H], U8, align_bytes=64)
        nc.vector.tensor_copy(
            ws_dealt[:].rearrange("p (w t m) -> p w t m", w=2, t=PACK),
            ws_rows[:].rearrange("p (w m t) -> p w t m", w=2, t=PACK),
        )
        move_scale_rows(nc.sync, ws_dealt, ws_dealt)

        xq_words = keep.tile([P, S], U32, align_bytes=64)
        nc.vector.tensor_copy(xq_words[:], x_table[:].indirect(offs_list[:]))
        xh_words = keep.tile([P, S], U32, align_bytes=64)
        nc.vector.tensor_copy(xh_words[:], x_table[:].indirect(hz_list[:]))
        w1_dealt = keep.tile([P, H], U32, tag="w1_then_cand_bytes", align_bytes=64)
        w2_dealt = keep.tile([P, H], U32, tag="w2_then_cand_words", align_bytes=64)
        for dealt, raw in ((w1_dealt, w1_raw), (w2_dealt, w2_raw)):
            nc.scalar.copy(
                dealt[:].rearrange("p (t m) -> p m t", t=PACK), raw[:].rearrange("p (m t) -> p m t", t=PACK)
            )

        y = []
        for t in range(PACK):
            cols = slice(t * P, (t + 1) * P)
            bank = psum.tile([P, S], F32, name=f"y_bank{t}", tag=f"bank{t}")
            for half, (dealt, words) in enumerate(((w1_dealt, xq_words), (w2_dealt, xh_words))):
                nc.tensor.matmul_mx(
                    out=bank[:],
                    lhsT=dealt[:, cols].bitcast(FP8X4),
                    lhsT_scale=ws_dealt[:, half * H + t * P : half * H + (t + 1) * P],
                    rhs=words[:].bitcast(FP8X4),
                    rhs_scale=picked_scale[:, half * S : (half + 1) * S],
                    start=(half == 0),
                    stop=(half == 1),
                )
            y_t = keep.tile([P, S], F32, name=f"y{t}")
            if t == 0:
                nc.scalar.activation(out=y_t[:], in_=bank[:], func=COPY)
            else:
                nc.vector.tensor_copy(y_t[:], bank[:])
            y.append(y_t)

        cand_list = load_list("cand_list", cand)
        n2_list = load_list("n2_list", n2)
        n3_list = load_list("n3_list", n3)
        n4_list = load_list("n4_list", n4)
        gain = keep.tile([P, PACK], F32, tag="w1_raw_then_gain", align_bytes=64)
        nc.sync.dma_start(out=gain[:], in_=gs.rearrange("(p t) o -> p (t o)", t=PACK))

        cand_words = keep.tile([P, C], U32, tag="w2_then_cand_words", align_bytes=64)
        nc.vector.tensor_copy(cand_words[:], x_table[:].indirect(cand_list[:]))

        ds = []
        for t in range(PACK):
            ds_t = keep.tile([P, 2 * S], F32, name=f"ds{t}")
            nc.scalar.activation(out=ds_t[:].indirect(n1_list[:]), in_=y[t][:], func=COPY)
            ds.append(ds_t)
        st = []
        for t in range(PACK):
            st_t = keep.tile([P, S], F32, name=f"st{t}")
            nc.vector.tensor_tensor(st_t[:], y[t][:], ds[t][:, 0:S], ALU.max)
            st.append(st_t)

        cand_bytes = keep.tile([P, C], U8, tag="w1_then_cand_bytes", align_bytes=64)
        nc.vector.tensor_copy(cand_bytes[:], xs_rows[:].indirect(cand_list[:]))
        cand_scale = keep.tile([P, C], U8, align_bytes=64)
        nc.vector.tensor_copy(cand_scale[:].bitcast(I32), cand_bytes[:].bitcast(I32))
        move_scale_rows(nc.sync, cand_scale, cand_bytes)

        z = keep.tile([P, S, PACK], BF16, align_bytes=64)
        z_codes = keep.tile([P, S], U32, align_bytes=64)
        z_scale = keep.tile([P, S], U8, align_bytes=64)
        halves = [slice(0, S // 2), slice(S // 2, S)]
        for t in range(PACK):
            ds2_t = keep.tile([P, 2 * S], F32, name=f"ds2_{t}")
            nc.scalar.activation(out=ds2_t[:].indirect(n2_list[:]), in_=st[t][:], func=COPY)
            diff = keep.tile([P, S], F32, name=f"diff{t}")
            pieces = halves if t == PACK - 1 else [slice(0, S)]
            for cols in pieces:
                nc.vector.tensor_tensor(diff[:, cols], st[t][:, cols], ds2_t[:, cols], ALU.subtract)
            for cols in pieces:
                nc.vector.tensor_scalar(z[:, cols, t], diff[:, cols], gain[:, t : t + 1], None, ALU.mult)
        for cols in halves:
            nc.vector.quantize_mx(
                out=z_codes[:, cols].bitcast(FP8X4),
                scales=z_scale[:, cols],
                in_=z[:, cols, :].rearrange("p j t -> p (j t)"),
            )

        scores, pairs = [], []
        for c in range(C // P):
            rows = slice(c * P, (c + 1) * P)
            s_c = keep.tile([P, S], F32, name=f"s{c}")
            pieces = halves if c == 0 else [slice(0, S)]
            for number, cols in enumerate(pieces):
                bank = psum.tile([P, cols.stop - cols.start], F32, name=f"s_bank{c}_{number}", tag=f"bank{c + number * PACK}")
                nc.tensor.matmul_mx(
                    out=bank[:],
                    lhsT=cand_words[:, rows].bitcast(FP8X4),
                    lhsT_scale=cand_scale[:, rows],
                    rhs=z_codes[:, cols].bitcast(FP8X4),
                    rhs_scale=z_scale[:, cols],
                    start=True,
                    stop=True,
                )
                if c == 0:
                    nc.scalar.activation(out=s_c[:, cols], in_=bank[:], func=COPY, scale=0.0625)
                else:
                    nc.vector.tensor_scalar(s_c[:, cols], bank[:], 0.0625, None, ALU.mult)
            scores.append(s_c)

        def fetch(c):
            pa = keep.tile([P, W], F32, name=f"pa{c}")
            nc.scalar.activation(out=pa[:], in_=scores[c][:].indirect(n3_list[:]), func=COPY)
            pb = keep.tile([P, W], F32, name=f"pb{c}")
            nc.scalar.activation(out=pb[:], in_=scores[c][:].indirect(n4_list[:]), func=COPY)
            ra = keep.tile([P, W], F32, name=f"ra{c}")
            nc.vector.tensor_tensor(ra[:], pa[:], pb[:], ALU.max)
            pairs.append(ra)

        def put_back(c):
            nc.scalar.activation(out=scores[c][:].indirect(n3_list[:]), in_=pairs[c][:], func=COPY)
            nc.sync.dma_start(out=out[c * P : (c + 1) * P, :], in_=scores[c][:])

        fetch(0)
        for c in range(1, C // P):
            fetch(c)
            put_back(c - 1)
        put_back(C // P - 1)
